import numpy as np
import ml_dtypes


def mxq(x, axis, fmt="e4m3"):
    dtype, down = {"e4m3": (ml_dtypes.float8_e4m3fn, 7), "e5m2": (ml_dtypes.float8_e5m2, 14)}[fmt]
    v = np.moveaxis(np.asarray(x, np.float32).astype(ml_dtypes.bfloat16).astype(np.float64), axis, -1)
    blocks = v.reshape(v.shape[:-1] + (-1, 32))
    amax = np.abs(blocks).max(-1, keepdims=True)
    byte = np.maximum(np.where(amax > 0, np.frexp(amax)[1] - 1 + 127, 0) - down, 1)
    scale = np.exp2(byte - 127.0)
    codes = (blocks / scale).astype(np.float32).astype(dtype).astype(np.float64)
    return np.moveaxis((codes * scale).reshape(v.shape), -1, axis)


WIDE = False


def mx_kscale(k):
    if not WIDE:
        return np.ones(k)
    levels = np.array([10, -10, 5, -5, 0])
    if k % 512:
        return np.exp2(np.random.permutation(np.resize(levels, k // 32))).repeat(32)
    a = np.empty((k // 512, 16))
    for p in range(k // 512):
        a[p, :8] = np.random.permutation(np.resize(levels, 8))
        for g in range(8):
            far = levels[np.abs(levels - a[p, g]) >= 10]
            a[p, g + 8] = far[np.random.randint(len(far))]
    return np.exp2(a.ravel()).repeat(32)


def f64(x):
    return np.asarray(x).astype(np.float64)


def striped8(idx):
    return np.asarray(idx).reshape(8, -1, 16).transpose(0, 2, 1).reshape(128, -1).astype(np.uint16)


def unstriped8(offs):
    return offs.reshape(8, 16, -1).transpose(0, 2, 1).reshape(8, -1).astype(np.int64)


def pick8(x, idx, run):
    r = np.arange(len(x))
    return x[r[:, None], idx[r % (8 * run) // run]]


E2M1 = np.array([0.0, 0.5, 1.0, 1.5, 2.0, 3.0, 4.0, 6.0, -0.0, -0.5, -1.0, -1.5, -2.0, -3.0, -4.0, -6.0])


def pack_weight(w, fmt):
    k, n = w.shape
    w = f64(np.asarray(w, np.float32).astype(ml_dtypes.bfloat16)).reshape(k // 32, 32, n)
    amax = np.abs(w).max(1)
    if fmt == "e4m3":
        byte = np.frexp(amax)[1] - 1 + 127 - 7
    else:
        mant, ex = np.frexp(amax / 6.0)
        byte = np.where(mant > 0.5, ex, ex - 1) + 127
    byte = np.clip(np.where(amax > 0, byte, 1), 1, 254)
    scaled = (w * np.exp2(127.0 - byte)[:, None, :]).reshape(k, n).astype(np.float32)
    by_word = np.ascontiguousarray(scaled.reshape(k // 512, 128, 4, n).transpose(0, 1, 3, 2))
    if fmt == "e4m3":
        words = by_word.astype(ml_dtypes.float8_e4m3fn).view(np.uint8)
    else:
        c = by_word.astype(ml_dtypes.float4_e2m1fn).view(np.uint8) & 0xF
        words = (c[..., 0::2] | (c[..., 1::2] << 4)).reshape(k // 512, 128, 2 * n)
    return np.ascontiguousarray(words), np.ascontiguousarray(byte.astype(np.uint8).reshape(k // 512, 16, n))


def unpack_weight(words, scales, fmt):
    g, _, n = scales.shape
    words = np.ascontiguousarray(words).reshape(g, 128, n, -1)
    if fmt == "e4m3":
        vals = words.view(ml_dtypes.float8_e4m3fn).astype(np.float64)
    else:
        nib = np.empty((g, 128, n, 4), np.uint8)
        nib[..., 0::2] = words & 0xF
        nib[..., 1::2] = words >> 4
        vals = E2M1[nib]
    vals = vals * np.repeat(np.exp2(scales.astype(np.float64) - 127.0), 8, axis=1)[..., None]
    return vals.transpose(0, 1, 3, 2).reshape(g * 512, n)


D, T, U, I, Q = 512, 1024, 1024, 512, 128


def setup_inputs():
    n = np.random.standard_normal
    idx = np.stack([np.random.permutation(T)[:I] for _ in range(8)])
    idx2 = np.stack([np.random.permutation(U)[:I] for _ in range(8)])
    idx3 = np.stack([np.random.permutation(T)[:I] for _ in range(8)])
    idx4 = np.stack([np.random.permutation(T)[:I] for _ in range(8)])
    idx5 = np.stack([np.random.permutation(U)[:I] for _ in range(8)])
    idx6 = np.stack([np.random.permutation(T)[:I] for _ in range(8)])
    fd = mx_kscale(D)
    keysp = pack_weight(n((D, T)) / fd[:, None], "e2m1")
    notesp = pack_weight(n((D, U)) / fd[:, None], "e4m3")
    return {
        "query": (n((D, Q)) * 1.0 / np.sqrt(D) * fd[:, None]).astype(np.float32),
        "keys_words": keysp[0],
        "keys_scales": keysp[1],
        "notes_words": notesp[0],
        "notes_scales": notesp[1],
        "offs": striped8(idx),
        "offs2": striped8(idx2),
        "offs3": striped8(idx3),
        "offs4": striped8(idx4),
        "offs5": striped8(idx5),
        "offs6": striped8(idx6),
    }


def reference(query, keys_words, keys_scales, notes_words, notes_scales, offs, offs2, offs3, offs4, offs5, offs6):
    idx = unstriped8(offs)
    idx2 = unstriped8(offs2)
    idx3 = unstriped8(offs3)
    idx4 = unstriped8(offs4)
    idx5 = unstriped8(offs5)
    idx6 = unstriped8(offs6)
    keysu = unpack_weight(keys_words, keys_scales, "e2m1")
    notesu = unpack_weight(notes_words, notes_scales, "e4m3")
    queryq = mxq(f64(query), 0, "e4m3")
    a = queryq.T @ keysu
    b = queryq.T @ notesu
    r = pick8(b, idx2, 16) - pick8(a, idx, 16)
    f1 = np.zeros((Q, T))
    f1[np.arange(Q)[:, None], idx[np.arange(Q) % 128 // 16]] = r
    a2 = a + f1
    v = np.maximum(pick8(a2, idx3, 16), pick8(b, idx5, 16))
    f2 = np.zeros((Q, T))
    f2[np.arange(Q)[:, None], idx4[np.arange(Q) % 128 // 16]] = v
    a3 = a2 + f2
    y = pick8(a3, idx6, 16)
    return y

@@ -1,0 +1,143 @@
+from contextlib import ExitStack
+
+import concourse.mybir as mybir
+
+D, T, U, I, Q = 512, 1024, 1024, 512, 128
+FLOPS = 2 * D * Q * (T + U)
+
+F32 = mybir.dt.float32
+BF16 = mybir.dt.bfloat16
+I32 = mybir.dt.int32
+U32 = mybir.dt.uint32
+U16 = mybir.dt.uint16
+U8 = mybir.dt.uint8
+FP8X4 = mybir.dt.float8_e4m3fn_x4
+FP4X4 = mybir.dt.float4_e2m1fn_x4
+ADD = mybir.AluOpType.add
+MAX = mybir.AluOpType.max
+COPY = mybir.ActivationFunctionType.Copy
+
+P = 128
+PACK = 4
+N_MM = 256
+HALF = I // 2
+LIST_COLS = I // 16
+
+
+def tile_attend_mendedtwice_two_kernel(
+    tc, query, keys_words, keys_scales, notes_words, notes_scales, offs, offs2, offs3, offs4, offs5, offs6, out
+):
+    nc = tc.nc
+    with ExitStack() as ctx:
+        lists = ctx.enter_context(tc.tile_pool(name="lists", bufs=1))
+        sb = ctx.enter_context(tc.tile_pool(name="sb", bufs=1))
+        psum = ctx.enter_context(tc.psum_pool(name="psum", bufs=1))
+
+        k_plane = sb.tile([P, T], U8, align_bytes=64)
+        n_plane = sb.tile([P, U], U8, align_bytes=64)
+        nc.vector.memset(k_plane[:].bitcast(I32), 0)
+        nc.vector.memset(n_plane[:].bitcast(I32), 0)
+
+        q_raw = sb.tile([P, PACK, Q], F32)
+        nc.sync.dma_start(q_raw[:], query.rearrange("(p j) q -> p j q", j=PACK))
+
+        def load_plane(plane, scales, queue):
+            for quad in range(4):
+                queue.dma_start(
+                    plane[32 * quad : 32 * quad + 4, :].bitcast(I32),
+                    scales[0, 4 * quad : 4 * quad + 4, :].bitcast(I32),
+                )
+
+        load_plane(k_plane, keys_scales, nc.sync)
+        k_words = sb.tile([P, 2 * T], U8, align_bytes=64)
+        nc.sync.dma_start(k_words[:].bitcast(I32), keys_words[0].bitcast(I32))
+        n_words = sb.tile([P, U], U32, align_bytes=64)
+        nc.sync.dma_start(n_words[:].bitcast(I32), notes_words[0].rearrange("p c r -> p (c r)").bitcast(I32))
+        load_plane(n_plane, notes_scales, nc.sync)
+
+        def load_list(name, src):
+            tile = lists.tile([P, LIST_COLS], U16, name=name)
+            nc.sync.dma_start(tile[:], src)
+            return tile
+
+        l1 = load_list("l1", offs)
+        l2 = load_list("l2", offs2)
+        l5 = load_list("l5", offs5)
+        l3 = load_list("l3", offs3)
+        l4 = load_list("l4", offs4)
+        l6 = load_list("l6", offs6)
+
+        def half(lst, h):
+            return lst[:, h * (LIST_COLS // 2) : (h + 1) * (LIST_COLS // 2)]
+
+        f1 = sb.tile([P, T], F32)
+        f2 = sb.tile([P, T], F32)
+        nc.vector.memset(f1[:], 0.0)
+        nc.vector.memset(f2[:], 0.0)
+
+        q_bf = sb.tile([P, Q, PACK], BF16, align_bytes=64)
+        q_turned = q_raw[:].rearrange("p j q -> p q j")
+        nc.vector.tensor_copy(q_bf[:, : Q // 2, :], q_turned[:, : Q // 2, :])
+        nc.scalar.activation(q_bf[:, Q // 2 :, :], q_turned[:, Q // 2 :, :], COPY)
+        q_words = sb.tile([P, Q], U32, align_bytes=64)
+        q_plane = sb.tile([P, Q], U8, align_bytes=64)
+        nc.vector.quantize_mx(q_words[:].bitcast(FP8X4), q_plane[:], q_bf[:].rearrange("p q j -> p (q j)"))
+
+        a = sb.tile([P, T], F32)
+        b = sb.tile([P, U], F32)
+        for c in range(T // N_MM):
+            cols = slice(c * N_MM, (c + 1) * N_MM)
+            bank = psum.tile([P, N_MM], F32, name=f"a_bank{c}")
+            nc.tensor.matmul_mx(
+                bank[:],
+                lhsT=q_words[:].bitcast(FP8X4),
+                lhsT_scale=q_plane[:],
+                rhs=k_words[:, 2 * c * N_MM : 2 * (c + 1) * N_MM].bitcast(FP4X4),
+                rhs_scale=k_plane[:, cols],
+                start=True,
+                stop=True,
+            )
+            nc.scalar.copy(a[:, cols], bank[:])
+        for c in range(U // N_MM):
+            cols = slice(c * N_MM, (c + 1) * N_MM)
+            bank = psum.tile([P, N_MM], F32, name=f"b_bank{c}")
+            nc.tensor.matmul_mx(
+                bank[:],
+                lhsT=q_words[:].bitcast(FP8X4),
+                lhsT_scale=q_plane[:],
+                rhs=n_words[:, cols].bitcast(FP8X4),
+                rhs_scale=n_plane[:, cols],
+                start=True,
+                stop=True,
+            )
+            nc.vector.tensor_copy(b[:, cols], bank[:])
+
+        minus_a = sb.tile([P, I], F32)
+        b_new = sb.tile([P, I], F32)
+        nc.scalar.activation(minus_a[:], a[:].indirect(l1[:]), COPY, scale=-1.0)
+        nc.vector.tensor_copy(b_new[:, :HALF], b[:].indirect(half(l2, 0)))
+        nc.scalar.activation(b_new[:, HALF:], b[:].indirect(half(l2, 1)), COPY)
+        nc.vector.tensor_tensor(f1[:].indirect(l1[:]), b_new[:], minus_a[:], ADD)
+        b_rival = sb.tile([P, I], F32)
+        nc.scalar.activation(b_rival[:], b[:].indirect(l5[:]), COPY)
+
+        a2 = sb.tile([P, T], F32)
+        nc.vector.tensor_tensor(a2[:], a[:], f1[:], ADD)
+
+        a2_picked = [sb.tile([P, HALF], F32, name=f"a2_picked{h}") for h in range(2)]
+        v = sb.tile([P, I], F32)
+        nc.vector.tensor_copy(a2_picked[0][:], a2[:].indirect(half(l3, 0)))
+        nc.scalar.activation(a2_picked[1][:], a2[:].indirect(half(l3, 1)), COPY)
+        for h in range(2):
+            cols = slice(h * HALF, (h + 1) * HALF)
+            nc.vector.tensor_tensor(v[:, cols], a2_picked[h][:], b_rival[:, cols], MAX)
+        nc.vector.tensor_copy(f2[:].indirect(l4[:]), v[:])
+
+        a3 = sb.tile([P, T], F32)
+        nc.vector.tensor_tensor(a3[:], a2[:], f2[:], ADD)
+
+        y = [sb.tile([P, HALF], F32, name=f"y{h}") for h in range(2)]
+        nc.vector.tensor_copy(y[0][:], a3[:].indirect(half(l6, 0)))
+        nc.sync.dma_start(out[:, :HALF], y[0][:])
+        nc.scalar.activation(y[1][:], a3[:].indirect(half(l6, 1)), COPY)
+        nc.scalar.dma_start(out[:, HALF:], y[1][:])

@@ -1,6 +1,7 @@
 from contextlib import ExitStack
 
 import concourse.mybir as mybir
+from concourse.masks import make_identity
 
 D, T, U, I, Q = 512, 1024, 1024, 512, 128
 FLOPS = 2 * D * Q * (T + U)
@@ -14,12 +15,15 @@ U8 = mybir.dt.uint8
 FP8X4 = mybir.dt.float8_e4m3fn_x4
 FP4X4 = mybir.dt.float4_e2m1fn_x4
 ADD = mybir.AluOpType.add
+MULT = mybir.AluOpType.mult
 MAX = mybir.AluOpType.max
 COPY = mybir.ActivationFunctionType.Copy
 
 P = 128
 PACK = 4
-N_MM = 256
+A_WIDTHS = (512, 256, 128, 128)
+B_WIDTHS = (256, 256, 256, 128, 128)
+SPLIT = 768
 HALF = I // 2
 LIST_COLS = I // 16
 
@@ -41,19 +45,20 @@ def tile_attend_mendedtwice_two_kernel(
         q_raw = sb.tile([P, PACK, Q], F32)
         nc.sync.dma_start(q_raw[:], query.rearrange("(p j) q -> p j q", j=PACK))
 
-        def load_plane(plane, scales, queue):
-            for quad in range(4):
-                queue.dma_start(
+        def load_plane(plane, scales, quads):
+            for quad in quads:
+                nc.sync.dma_start(
                     plane[32 * quad : 32 * quad + 4, :].bitcast(I32),
                     scales[0, 4 * quad : 4 * quad + 4, :].bitcast(I32),
                 )
 
-        load_plane(k_plane, keys_scales, nc.sync)
+        load_plane(k_plane, keys_scales, (0, 1))
         k_words = sb.tile([P, 2 * T], U8, align_bytes=64)
         nc.sync.dma_start(k_words[:].bitcast(I32), keys_words[0].bitcast(I32))
-        n_words = sb.tile([P, U], U32, align_bytes=64)
+        load_plane(k_plane, keys_scales, (2, 3))
+        n_words = sb.tile([P, 4 * U], U8, align_bytes=64)
         nc.sync.dma_start(n_words[:].bitcast(I32), notes_words[0].rearrange("p c r -> p (c r)").bitcast(I32))
-        load_plane(n_plane, notes_scales, nc.sync)
+        load_plane(n_plane, notes_scales, range(4))
 
         def load_list(name, src):
             tile = lists.tile([P, LIST_COLS], U16, name=name)
@@ -75,7 +80,7 @@ def tile_attend_mendedtwice_two_kernel(
         nc.vector.memset(f1[:], 0.0)
         nc.vector.memset(f2[:], 0.0)
 
-        q_bf = sb.tile([P, Q, PACK], BF16, align_bytes=64)
+        q_bf = sb.tile([P, Q, PACK], BF16, align_bytes=64, tag="q_bf_then_ident")
         q_turned = q_raw[:].rearrange("p j q -> p q j")
         nc.vector.tensor_copy(q_bf[:, : Q // 2, :], q_turned[:, : Q // 2, :])
         nc.scalar.activation(q_bf[:, Q // 2 :, :], q_turned[:, Q // 2 :, :], COPY)
@@ -83,38 +88,44 @@ def tile_attend_mendedtwice_two_kernel(
         q_plane = sb.tile([P, Q], U8, align_bytes=64)
         nc.vector.quantize_mx(q_words[:].bitcast(FP8X4), q_plane[:], q_bf[:].rearrange("p q j -> p (q j)"))
 
+        ident = sb.tile([P, P], F32, align_bytes=64, tag="q_bf_then_ident")
+        make_identity(nc, ident[:])
+
         a = sb.tile([P, T], F32)
         b = sb.tile([P, U], F32)
-        for c in range(T // N_MM):
-            cols = slice(c * N_MM, (c + 1) * N_MM)
-            bank = psum.tile([P, N_MM], F32, name=f"a_bank{c}")
+
+        def product(bank_name, words, dtype, bytes_per_col, plane, start, width):
+            bank = psum.tile([P, width], F32, name=bank_name)
             nc.tensor.matmul_mx(
                 bank[:],
                 lhsT=q_words[:].bitcast(FP8X4),
                 lhsT_scale=q_plane[:],
-                rhs=k_words[:, 2 * c * N_MM : 2 * (c + 1) * N_MM].bitcast(FP4X4),
-                rhs_scale=k_plane[:, cols],
+                rhs=words[:, bytes_per_col * start : bytes_per_col * (start + width)].bitcast(dtype),
+                rhs_scale=plane[:, start : start + width],
                 start=True,
                 stop=True,
             )
-            nc.scalar.copy(a[:, cols], bank[:])
-        for c in range(U // N_MM):
-            cols = slice(c * N_MM, (c + 1) * N_MM)
-            bank = psum.tile([P, N_MM], F32, name=f"b_bank{c}")
-            nc.tensor.matmul_mx(
-                bank[:],
-                lhsT=q_words[:].bitcast(FP8X4),
-                lhsT_scale=q_plane[:],
-                rhs=n_words[:, cols].bitcast(FP8X4),
-                rhs_scale=n_plane[:, cols],
-                start=True,
-                stop=True,
-            )
-            nc.vector.tensor_copy(b[:, cols], bank[:])
+            return bank
+
+        a_banks = []
+        start = 0
+        for c, width in enumerate(A_WIDTHS):
+            bank = product(f"bank{c}", k_words, FP4X4, 2, k_plane, start, width)
+            a_banks.append(bank)
+            if c in (0, 3):
+                nc.vector.tensor_copy(a[:, start : start + width], bank[:])
+            else:
+                nc.scalar.copy(a[:, start : start + width], bank[:])
+            start += width
+        start = 0
+        for c, width in enumerate(B_WIDTHS):
+            bank = product(f"bank{(4, 5, 6, 7, 2)[c]}", n_words, FP8X4, 4, n_plane, start, width)
+            nc.scalar.copy(b[:, start : start + width], bank[:])
+            start += width
 
         minus_a = sb.tile([P, I], F32)
         b_new = sb.tile([P, I], F32)
-        nc.scalar.activation(minus_a[:], a[:].indirect(l1[:]), COPY, scale=-1.0)
+        nc.vector.tensor_scalar(minus_a[:], a[:].indirect(l1[:]), -1.0, 0.0, MULT, ADD)
         nc.vector.tensor_copy(b_new[:, :HALF], b[:].indirect(half(l2, 0)))
         nc.scalar.activation(b_new[:, HALF:], b[:].indirect(half(l2, 1)), COPY)
         nc.vector.tensor_tensor(f1[:].indirect(l1[:]), b_new[:], minus_a[:], ADD)
@@ -122,7 +133,12 @@ def tile_attend_mendedtwice_two_kernel(
         nc.scalar.activation(b_rival[:], b[:].indirect(l5[:]), COPY)
 
         a2 = sb.tile([P, T], F32)
-        nc.vector.tensor_tensor(a2[:], a[:], f1[:], ADD)
+        start = 0
+        for bank, width in zip(a_banks, A_WIDTHS[:2]):
+            cols = slice(start, start + width)
+            nc.vector.tensor_tensor(a2[:, cols], bank[:], f1[:, cols], ADD)
+            start += width
+        nc.gpsimd.tensor_tensor(a2[:, SPLIT:], a[:, SPLIT:], f1[:, SPLIT:], ADD)
 
         a2_picked = [sb.tile([P, HALF], F32, name=f"a2_picked{h}") for h in range(2)]
         v = sb.tile([P, I], F32)
@@ -134,7 +150,23 @@ def tile_attend_mendedtwice_two_kernel(
         nc.vector.tensor_copy(f2[:].indirect(l4[:]), v[:])
 
         a3 = sb.tile([P, T], F32)
-        nc.vector.tensor_tensor(a3[:], a2[:], f2[:], ADD)
+        a2_turned = sb.tile([P, SPLIT], F32)
+        start = 0
+        for c, width in enumerate(A_WIDTHS[:2]):
+            bank = psum.tile([P, width], F32, name=f"bank{4 + c}")
+            for blk in range(0, width, P):
+                nc.tensor.transpose(bank[:, blk : blk + P], a2[:, start + blk : start + blk + P], ident[:])
+            nc.scalar.copy(a2_turned[:, start : start + width], bank[:])
+            start += width
+        start = 0
+        for c, width in enumerate(A_WIDTHS[:2]):
+            cols = slice(start, start + width)
+            bank = psum.tile([P, width], F32, name=f"bank{6 + c}")
+            for blk in range(0, width, P):
+                nc.tensor.transpose(bank[:, blk : blk + P], a2_turned[:, start + blk : start + blk + P], ident[:])
+            nc.vector.tensor_tensor(a3[:, cols], bank[:], f2[:, cols], ADD)
+            start += width
+        nc.gpsimd.tensor_tensor(a3[:, SPLIT:], a2[:, SPLIT:], f2[:, SPLIT:], ADD)
 
         y = [sb.tile([P, HALF], F32, name=f"y{h}") for h in range(2)]
         nc.vector.tensor_copy(y[0][:], a3[:].indirect(half(l6, 0)))

from contextlib import ExitStack

import concourse.mybir as mybir
from concourse.masks import make_identity

D, T, U, I, Q = 512, 1024, 1024, 512, 128
FLOPS = 2 * D * Q * (T + U)

F32 = mybir.dt.float32
BF16 = mybir.dt.bfloat16
I32 = mybir.dt.int32
U32 = mybir.dt.uint32
U16 = mybir.dt.uint16
U8 = mybir.dt.uint8
FP8X4 = mybir.dt.float8_e4m3fn_x4
FP4X4 = mybir.dt.float4_e2m1fn_x4
ADD = mybir.AluOpType.add
MULT = mybir.AluOpType.mult
MAX = mybir.AluOpType.max
COPY = mybir.ActivationFunctionType.Copy

P = 128
PACK = 4
A_WIDTHS = (512, 256, 128, 128)
B_WIDTHS = (256, 256, 256, 128, 128)
SPLIT = 768
HALF = I // 2
LIST_COLS = I // 16


def tile_attend_mendedtwice_two_kernel(
    tc, query, keys_words, keys_scales, notes_words, notes_scales, offs, offs2, offs3, offs4, offs5, offs6, out
):
    nc = tc.nc
    with ExitStack() as ctx:
        lists = ctx.enter_context(tc.tile_pool(name="lists", bufs=1))
        sb = ctx.enter_context(tc.tile_pool(name="sb", bufs=1))
        psum = ctx.enter_context(tc.psum_pool(name="psum", bufs=1))

        k_plane = sb.tile([P, T], U8, align_bytes=64)
        n_plane = sb.tile([P, U], U8, align_bytes=64)
        nc.vector.memset(k_plane[:].bitcast(I32), 0)
        nc.vector.memset(n_plane[:].bitcast(I32), 0)

        q_raw = sb.tile([P, PACK, Q], F32)
        nc.sync.dma_start(q_raw[:], query.rearrange("(p j) q -> p j q", j=PACK))

        def load_plane(plane, scales, quads):
            for quad in quads:
                nc.sync.dma_start(
                    plane[32 * quad : 32 * quad + 4, :].bitcast(I32),
                    scales[0, 4 * quad : 4 * quad + 4, :].bitcast(I32),
                )

        load_plane(k_plane, keys_scales, (0, 1))
        k_words = sb.tile([P, 2 * T], U8, align_bytes=64)
        nc.sync.dma_start(k_words[:].bitcast(I32), keys_words[0].bitcast(I32))
        load_plane(k_plane, keys_scales, (2, 3))
        n_words = sb.tile([P, 4 * U], U8, align_bytes=64)
        nc.sync.dma_start(n_words[:].bitcast(I32), notes_words[0].rearrange("p c r -> p (c r)").bitcast(I32))
        load_plane(n_plane, notes_scales, range(4))

        def load_list(name, src):
            tile = lists.tile([P, LIST_COLS], U16, name=name)
            nc.sync.dma_start(tile[:], src)
            return tile

        l1 = load_list("l1", offs)
        l2 = load_list("l2", offs2)
        l5 = load_list("l5", offs5)
        l3 = load_list("l3", offs3)
        l4 = load_list("l4", offs4)
        l6 = load_list("l6", offs6)

        def half(lst, h):
            return lst[:, h * (LIST_COLS // 2) : (h + 1) * (LIST_COLS // 2)]

        f1 = sb.tile([P, T], F32)
        f2 = sb.tile([P, T], F32)
        nc.vector.memset(f1[:], 0.0)
        nc.vector.memset(f2[:], 0.0)

        q_bf = sb.tile([P, Q, PACK], BF16, align_bytes=64, tag="q_bf_then_ident")
        q_turned = q_raw[:].rearrange("p j q -> p q j")
        nc.vector.tensor_copy(q_bf[:, : Q // 2, :], q_turned[:, : Q // 2, :])
        nc.scalar.activation(q_bf[:, Q // 2 :, :], q_turned[:, Q // 2 :, :], COPY)
        q_words = sb.tile([P, Q], U32, align_bytes=64)
        q_plane = sb.tile([P, Q], U8, align_bytes=64)
        nc.vector.quantize_mx(q_words[:].bitcast(FP8X4), q_plane[:], q_bf[:].rearrange("p q j -> p (q j)"))

        ident = sb.tile([P, P], F32, align_bytes=64, tag="q_bf_then_ident")
        make_identity(nc, ident[:])

        a = sb.tile([P, T], F32)
        b = sb.tile([P, U], F32)

        def product(bank_name, words, dtype, bytes_per_col, plane, start, width):
            bank = psum.tile([P, width], F32, name=bank_name)
            nc.tensor.matmul_mx(
                bank[:],
                lhsT=q_words[:].bitcast(FP8X4),
                lhsT_scale=q_plane[:],
                rhs=words[:, bytes_per_col * start : bytes_per_col * (start + width)].bitcast(dtype),
                rhs_scale=plane[:, start : start + width],
                start=True,
                stop=True,
            )
            return bank

        a_banks = []
        start = 0
        for c, width in enumerate(A_WIDTHS):
            bank = product(f"bank{c}", k_words, FP4X4, 2, k_plane, start, width)
            a_banks.append(bank)
            if c in (0, 3):
                nc.vector.tensor_copy(a[:, start : start + width], bank[:])
            else:
                nc.scalar.copy(a[:, start : start + width], bank[:])
            start += width
        start = 0
        for c, width in enumerate(B_WIDTHS):
            bank = product(f"bank{(4, 5, 6, 7, 2)[c]}", n_words, FP8X4, 4, n_plane, start, width)
            nc.scalar.copy(b[:, start : start + width], bank[:])
            start += width

        minus_a = sb.tile([P, I], F32)
        b_new = sb.tile([P, I], F32)
        nc.vector.tensor_scalar(minus_a[:], a[:].indirect(l1[:]), -1.0, 0.0, MULT, ADD)
        nc.vector.tensor_copy(b_new[:, :HALF], b[:].indirect(half(l2, 0)))
        nc.scalar.activation(b_new[:, HALF:], b[:].indirect(half(l2, 1)), COPY)
        nc.vector.tensor_tensor(f1[:].indirect(l1[:]), b_new[:], minus_a[:], ADD)
        b_rival = sb.tile([P, I], F32)
        nc.scalar.activation(b_rival[:], b[:].indirect(l5[:]), COPY)

        a2 = sb.tile([P, T], F32)
        start = 0
        for bank, width in zip(a_banks, A_WIDTHS[:2]):
            cols = slice(start, start + width)
            nc.vector.tensor_tensor(a2[:, cols], bank[:], f1[:, cols], ADD)
            start += width
        nc.gpsimd.tensor_tensor(a2[:, SPLIT:], a[:, SPLIT:], f1[:, SPLIT:], ADD)

        a2_picked = [sb.tile([P, HALF], F32, name=f"a2_picked{h}") for h in range(2)]
        v = sb.tile([P, I], F32)
        nc.vector.tensor_copy(a2_picked[0][:], a2[:].indirect(half(l3, 0)))
        nc.scalar.activation(a2_picked[1][:], a2[:].indirect(half(l3, 1)), COPY)
        for h in range(2):
            cols = slice(h * HALF, (h + 1) * HALF)
            nc.vector.tensor_tensor(v[:, cols], a2_picked[h][:], b_rival[:, cols], MAX)
        nc.vector.tensor_copy(f2[:].indirect(l4[:]), v[:])

        a3 = sb.tile([P, T], F32)
        a2_turned = sb.tile([P, SPLIT], F32)
        start = 0
        for c, width in enumerate(A_WIDTHS[:2]):
            bank = psum.tile([P, width], F32, name=f"bank{4 + c}")
            for blk in range(0, width, P):
                nc.tensor.transpose(bank[:, blk : blk + P], a2[:, start + blk : start + blk + P], ident[:])
            nc.scalar.copy(a2_turned[:, start : start + width], bank[:])
            start += width
        start = 0
        for c, width in enumerate(A_WIDTHS[:2]):
            cols = slice(start, start + width)
            bank = psum.tile([P, width], F32, name=f"bank{6 + c}")
            for blk in range(0, width, P):
                nc.tensor.transpose(bank[:, blk : blk + P], a2_turned[:, start + blk : start + blk + P], ident[:])
            nc.vector.tensor_tensor(a3[:, cols], bank[:], f2[:, cols], ADD)
            start += width
        nc.gpsimd.tensor_tensor(a3[:, SPLIT:], a2[:, SPLIT:], f2[:, SPLIT:], ADD)

        y = [sb.tile([P, HALF], F32, name=f"y{h}") for h in range(2)]
        nc.vector.tensor_copy(y[0][:], a3[:].indirect(half(l6, 0)))
        nc.sync.dma_start(out[:, :HALF], y[0][:])
        nc.scalar.activation(y[1][:], a3[:].indirect(half(l6, 1)), COPY)
        nc.scalar.dma_start(out[:, HALF:], y[1][:])
